import numpy as np
import ml_dtypes


def mxq(x, axis, fmt="e4m3"):
    dtype, down = {"e4m3": (ml_dtypes.float8_e4m3fn, 7), "e5m2": (ml_dtypes.float8_e5m2, 14)}[fmt]
    v = np.moveaxis(np.asarray(x, np.float32).astype(ml_dtypes.bfloat16).astype(np.float64), axis, -1)
    blocks = v.reshape(v.shape[:-1] + (-1, 32))
    amax = np.abs(blocks).max(-1, keepdims=True)
    byte = np.maximum(np.where(amax > 0, np.frexp(amax)[1] - 1 + 127, 0) - down, 1)
    scale = np.exp2(byte - 127.0)
    codes = (blocks / scale).astype(np.float32).astype(dtype).astype(np.float64)
    return np.moveaxis((codes * scale).reshape(v.shape), -1, axis)


WIDE = False


def mx_kscale(k):
    if not WIDE:
        return np.ones(k)
    levels = np.array([10, -10, 5, -5, 0])
    if k % 512:
        return np.exp2(np.random.permutation(np.resize(levels, k // 32))).repeat(32)
    a = np.empty((k // 512, 16))
    for p in range(k // 512):
        a[p, :8] = np.random.permutation(np.resize(levels, 8))
        for g in range(8):
            far = levels[np.abs(levels - a[p, g]) >= 10]
            a[p, g + 8] = far[np.random.randint(len(far))]
    return np.exp2(a.ravel()).repeat(32)


def f64(x):
    return np.asarray(x).astype(np.float64)


def striped(idx):
    return np.tile(idx.reshape(-1, 16).T, (8, 1)).astype(np.uint16)


def unstriped(offs):
    return offs[:16].T.reshape(-1).astype(np.int64)


def striped8(idx):
    return np.concatenate([x.reshape(-1, 16).T for x in idx]).astype(np.uint16)


def runs(offs, k):
    lists = np.stack([offs[16 * r : 16 * r + 16].T.reshape(-1) for r in range(8)]).astype(np.int64)
    return lists[np.arange(k) % 512 // 64]


def pack_weight(w):
    k, n = w.shape
    w = f64(np.asarray(w, np.float32).astype(ml_dtypes.bfloat16)).reshape(k // 32, 32, n)
    amax = np.abs(w).max(1)
    byte = np.clip(np.where(amax > 0, np.frexp(amax)[1] - 1 + 127 - 7, 1), 1, 254)
    scaled = (w * np.exp2(127.0 - byte)[:, None, :]).reshape(k, n).astype(np.float32)
    words = np.ascontiguousarray(scaled.reshape(k // 512, 128, 4, n).transpose(0, 1, 3, 2)).astype(ml_dtypes.float8_e4m3fn).view(np.uint8)
    return words, np.ascontiguousarray(byte.astype(np.uint8).reshape(k // 512, 16, n))


def unpack_weight(words, scales):
    g, p, n, _ = words.shape
    vals = np.ascontiguousarray(words).view(ml_dtypes.float8_e4m3fn).astype(np.float64) * np.repeat(np.exp2(scales.astype(np.float64) - 127.0), 8, axis=1)[..., None]
    return vals.transpose(0, 1, 3, 2).reshape(g * 512, n)


def sigmoid(v):
    return 1.0 / (1.0 + np.exp(-np.maximum(v, -700.0)))


K, T, S, N, G, H, W = 512, 2048, 512, 512, 2048, 512, 384


def setup_inputs():
    n = np.random.standard_normal
    s = mx_kscale(K)[:, None]
    u = mx_kscale(S)
    packed_xT = pack_weight(n((K, T)) * s)
    packed_dT = pack_weight(n((K, G)) / s)
    return {
        "x_words": packed_xT[0],
        "x_scales": packed_xT[1],
        "d_words": packed_dT[0],
        "d_scales": packed_dT[1],
        "gn": (np.random.uniform(0.5, 1.5, (H, 1)) * u[:, None]).astype(np.float32),
        "w1": (n((H, N)) / np.sqrt(H) / u[:, None]).astype(np.float32),
        "offs": striped(np.random.permutation(T)[:S]),
        "k1": striped8(np.random.randint(0, G, (8, H))),
        "n1": striped(np.random.permutation(S)[:W]),
        "n2": striped(np.random.permutation(S)[:W]),
        "n3": striped8(np.stack([np.random.permutation(S) for _ in range(8)])),
    }


def reference(x_words, x_scales, d_words, d_scales, gn, w1, offs, k1, n1, n2, n3):
    d_k1 = unpack_weight(d_words, d_scales)[np.arange(K)[:, None], runs(k1, K)]
    xq = unpack_weight(x_words, x_scales)[:, unstriped(offs)]
    h = 0.0625 * (d_k1.T @ xq)
    pa = h[:, unstriped(n2)]
    old = h[:, unstriped(n1)]
    ra = np.minimum(pa, old) - (0.5 * pa)
    ds = h.copy()
    ds[:, unstriped(n1)] = ra
    z = f64(gn) * ds
    h2 = mxq(f64(w1), 0, "e4m3").T @ mxq(z, 0, "e4m3")
    return h2 * (sigmoid(h2[np.arange(N)[:, None], runs(n3, N)]))

@@ -1,0 +1,193 @@
+from contextlib import ExitStack
+
+import concourse.mybir as mybir
+
+K, T, S, N, G, H, W = 512, 2048, 512, 512, 2048, 512, 384
+FLOPS = 2 * K * H * S + 2 * H * N * S
+
+F32 = mybir.dt.float32
+BF16 = mybir.dt.bfloat16
+I32 = mybir.dt.int32
+U32 = mybir.dt.uint32
+U16 = mybir.dt.uint16
+U8 = mybir.dt.uint8
+FP8X4 = mybir.dt.float8_e4m3fn_x4
+ALU = mybir.AluOpType
+ACT = mybir.ActivationFunctionType
+
+P = 128
+PACK = 4
+HALF = S // 2
+
+
+def tile_picked_pqlaykmingate_none_p_kernel(tc, x_words, x_scales, d_words, d_scales, gn, w1, offs, k1, n1, n2, n3, out):
+    nc = tc.nc
+    with ExitStack() as ctx:
+        lists = ctx.enter_context(tc.tile_pool(name="lists", bufs=1))
+        keep = ctx.enter_context(tc.tile_pool(name="keep", bufs=1))
+        psum = ctx.enter_context(tc.psum_pool(name="psum", bufs=1))
+
+        k1_t = lists.tile([P, H // 16], U16, name="k1_t")
+        offs_t = lists.tile([P, S // 16], U16, name="offs_t")
+        n1_t = lists.tile([P, W // 16], U16, name="n1_t")
+        n2_t = lists.tile([P, W // 16], U16, name="n2_t")
+        n3_t = lists.tile([P, S // 16], U16, name="n3_t")
+
+        d_bytes = keep.tile([P, G], U8, name="d_bytes", align_bytes=64)
+        x_bytes = keep.tile([P, T], U8, name="x_bytes", align_bytes=64)
+        d_table = keep.tile([P, G], I32, name="d_table", align_bytes=64)
+        x_table = keep.tile([P, T], I32, name="x_table", align_bytes=64)
+        gain = keep.tile([P, PACK], F32, name="gain")
+
+        nc.sync.dma_start(k1_t[:], k1)
+        nc.sync.dma_start(d_bytes[:].bitcast(I32), d_scales[0].bitcast(I32).unsqueeze(1).to_broadcast([16, 8, G // 4]))
+        nc.sync.dma_start(offs_t[:], offs)
+        for q in range(4):
+            nc.sync.dma_start(
+                x_bytes[32 * q : 32 * q + 32, :].bitcast(I32),
+                x_scales[0, 4 * q : 4 * q + 4, :].bitcast(I32).unsqueeze(0).to_broadcast([8, 4, T // 4]),
+            )
+        nc.sync.dma_start(d_table[:], d_words[0].rearrange("p c r -> p (c r)").bitcast(I32))
+        nc.sync.dma_start(n2_t[:], n2)
+        nc.sync.dma_start(n1_t[:], n1)
+        nc.sync.dma_start(x_table[:], x_words[0].rearrange("p c r -> p (c r)").bitcast(I32))
+        nc.sync.dma_start(n3_t[:], n3)
+        nc.sync.dma_start(gain[:], gn.rearrange("(p t) o -> p (t o)", t=PACK))
+        w_raw = []
+        for hf in range(2):
+            raw = keep.tile([P, PACK, N // 2], F32, name=f"w_raw{hf}")
+            nc.sync.dma_start(raw[:], w1[:, hf * (N // 2) : (hf + 1) * (N // 2)].rearrange("(p j) m -> p j m", j=PACK))
+            w_raw.append(raw)
+
+        d_picked_bytes = keep.tile([P, H], U8, name="d_picked_bytes", align_bytes=64)
+        nc.vector.tensor_copy(d_picked_bytes[:], d_bytes[:].indirect(k1_t[:]))
+        d_dealt_bytes = keep.tile([P, H], U8, name="d_dealt_bytes", align_bytes=64)
+        nc.vector.tensor_copy(
+            d_dealt_bytes[:].rearrange("p (t m) -> p m t", t=PACK), d_picked_bytes[:].rearrange("p (m t) -> p m t", t=PACK)
+        )
+        d_plane = keep.tile([P, H], U8, name="d_plane", align_bytes=64)
+        nc.vector.tensor_copy(d_plane[:].bitcast(I32), d_dealt_bytes[:].bitcast(I32))
+        for a in range(1, 4):
+            nc.scalar.dma_start(d_plane[a:P:32, :].bitcast(I32), d_dealt_bytes[8 * a : P : 32, :].bitcast(I32))
+
+        x_plane = keep.tile([P, S], U8, name="x_plane", align_bytes=64)
+        nc.vector.tensor_copy(x_plane[:], x_bytes[:].indirect(offs_t[:]))
+
+        d_picked = keep.tile([P, H], U32, name="d_picked", align_bytes=64)
+        nc.vector.tensor_copy(d_picked[:], d_table[:].bitcast(U32).indirect(k1_t[:]))
+        d_codes = keep.tile([P, H], U32, name="d_codes", align_bytes=64)
+        nc.vector.tensor_copy(
+            d_codes[:].bitcast(I32).rearrange("p (t m) -> p m t", t=PACK),
+            d_picked[:].bitcast(I32).rearrange("p (m t) -> p m t", t=PACK),
+        )
+        x_codes = keep.tile([P, S], U32, name="x_codes", align_bytes=64)
+        nc.vector.tensor_copy(x_codes[:], x_table[:].bitcast(U32).indirect(offs_t[:]))
+
+        h_acc = []
+        for t in range(PACK):
+            acc = psum.tile([P, S], F32, name=f"h_acc{t}")
+            cols = slice(t * P, (t + 1) * P)
+            nc.tensor.matmul_mx(
+                out=acc[:], lhsT=d_codes[:, cols].bitcast(FP8X4), lhsT_scale=d_plane[:, cols],
+                rhs=x_codes[:].bitcast(FP8X4), rhs_scale=x_plane[:], start=True, stop=True,
+            )
+            h_acc.append(acc)
+
+        w_bf = keep.tile([P, N * PACK], BF16, name="w_bf", align_bytes=64)
+
+        def cast_w(hf):
+            nc.vector.tensor_copy(
+                w_bf[:].rearrange("p (t a b j) -> p t a b j", t=PACK, b=8, j=PACK)[:, :, 8 * hf : 8 * hf + 8],
+                w_raw[hf][:].rearrange("p j (a t b) -> p t a b j", t=PACK, b=8),
+            )
+
+        h = [keep.tile([P, S], F32, name=f"h{t}") for t in range(PACK)]
+        q = [keep.tile([P, W], F32, name=f"q{t}") for t in range(PACK)]
+        dd = [keep.tile([P, W], F32, name=f"dd{t}") for t in range(PACK)]
+        ra = [keep.tile([P, W], F32, name=f"ra{t}") for t in range(PACK)]
+        z_pairs = keep.tile([P, 2, S, 2], BF16, name="z_pairs", align_bytes=64)
+
+        def leave_scalar(t):
+            nc.scalar.activation(h[t][:], h_acc[t][:], ACT.Copy, scale=0.0625)
+
+        def leave_vector(t):
+            nc.vector.tensor_scalar(h[t][:], h_acc[t][:], 0.0625, None, ALU.mult)
+
+        def fetch_pa(t):
+            nc.scalar.activation(q[t][:], h[t][:].indirect(n2_t[:]), ACT.Copy, scale=-0.5)
+
+        def new_values(t):
+            nc.vector.tensor_tensor(dd[t][:], h[t][:].indirect(n1_t[:]), q[t][:], ALU.add)
+            nc.vector.scalar_tensor_tensor(ra[t][:], q[t][:], -1.0, dd[t][:], ALU.mult, ALU.min)
+
+        def put_scalar(t):
+            nc.scalar.activation(h[t][:].indirect(n1_t[:]), ra[t][:], ACT.Copy)
+
+        def put_vector(t):
+            nc.vector.tensor_copy(h[t][:].indirect(n1_t[:]), ra[t][:])
+
+        def round_z(t):
+            nc.vector.tensor_scalar(z_pairs[:, t // 2, :, t % 2], h[t][:], gain[:, t : t + 1], None, ALU.mult)
+
+        cast_w(0)
+        leave_scalar(0)
+        fetch_pa(0)
+        leave_vector(1)
+        fetch_pa(1)
+        leave_scalar(2)
+        new_values(0)
+        leave_vector(3)
+        fetch_pa(2)
+        fetch_pa(3)
+        new_values(1)
+        put_scalar(0)
+        new_values(2)
+        put_scalar(1)
+        new_values(3)
+        put_scalar(2)
+        put_vector(3)
+        cast_w(1)
+        w_codes = keep.tile([P, N], U32, name="w_codes", align_bytes=64)
+        w_plane = keep.tile([P, N], U8, name="w_plane", align_bytes=64)
+        round_z(0)
+        nc.vector.quantize_mx(out=w_codes[:].bitcast(FP8X4), scales=w_plane[:], in_=w_bf[:])
+        round_z(1)
+        round_z(3)
+        round_z(2)
+
+        z_bf, z_codes, z_plane = [], [], []
+        for hf in range(2):
+            zb = keep.tile([P, HALF * PACK], BF16, name=f"z_bf{hf}", align_bytes=64)
+            nc.vector.tensor_copy(
+                zb[:].bitcast(F32).rearrange("p (c u) -> p c u", u=2),
+                z_pairs[:].rearrange("p u c e -> p u (c e)").bitcast(F32)[:, :, hf * HALF : (hf + 1) * HALF].rearrange("p u c -> p c u"),
+            )
+            z_bf.append(zb)
+        for hf in range(2):
+            zc = keep.tile([P, HALF], U32, name=f"z_codes{hf}", align_bytes=64)
+            zs = keep.tile([P, HALF], U8, name=f"z_plane{hf}", align_bytes=64)
+            nc.vector.quantize_mx(out=zc[:].bitcast(FP8X4), scales=zs[:], in_=z_bf[hf][:])
+            z_codes.append(zc)
+            z_plane.append(zs)
+
+        h2_acc = [psum.tile([P, S], F32, name=f"h2_acc{t}") for t in range(PACK)]
+        for t in range(PACK):
+            cols = slice(t * P, (t + 1) * P)
+            for hf in range(2):
+                nc.tensor.matmul_mx(
+                    out=h2_acc[t][:, hf * HALF : (hf + 1) * HALF], lhsT=w_codes[:, cols].bitcast(FP8X4), lhsT_scale=w_plane[:, cols],
+                    rhs=z_codes[hf][:].bitcast(FP8X4), rhs_scale=z_plane[hf][:], start=True, stop=True,
+                )
+
+        out_rows = out.rearrange("(a t b) n -> t a b n", t=PACK, b=8)
+        h2 = [keep.tile([P, S], F32, name=f"h2_{t}") for t in range(PACK)]
+        for t in range(PACK):
+            nc.vector.tensor_copy(h2[t][:], h2_acc[t][:])
+        for t in range(PACK):
+            for hf in range(2):
+                cols = slice(hf * HALF, (hf + 1) * HALF)
+                gate = keep.tile([P, HALF], F32, name=f"gate{t}_{hf}")
+                nc.scalar.activation(gate[:], h2[t][:].indirect(n3_t[:, 16 * hf : 16 * hf + 16]), ACT.Sigmoid)
+                res = keep.tile([P, HALF], F32, name=f"res{t}_{hf}")
+                nc.vector.tensor_tensor(res[:], h2[t][:, cols], gate[:], ALU.mult)
+                nc.sync.dma_start(out_rows[t, :, :, cols], res[:])

@@ -18,6 +18,7 @@ ACT = mybir.ActivationFunctionType
 P = 128
 PACK = 4
 HALF = S // 2
+SPLIT = 192
 
 
 def tile_picked_pqlaykmingate_none_p_kernel(tc, x_words, x_scales, d_words, d_scales, gn, w1, offs, k1, n1, n2, n3, out):
@@ -52,142 +53,129 @@ def tile_picked_pqlaykmingate_none_p_kernel(tc, x_words, x_scales, d_words, d_sc
         nc.sync.dma_start(n1_t[:], n1)
         nc.sync.dma_start(x_table[:], x_words[0].rearrange("p c r -> p (c r)").bitcast(I32))
         nc.sync.dma_start(n3_t[:], n3)
-        nc.sync.dma_start(gain[:], gn.rearrange("(p t) o -> p (t o)", t=PACK))
-        w_raw = []
-        for hf in range(2):
-            raw = keep.tile([P, PACK, N // 2], F32, name=f"w_raw{hf}")
-            nc.sync.dma_start(raw[:], w1[:, hf * (N // 2) : (hf + 1) * (N // 2)].rearrange("(p j) m -> p j m", j=PACK))
-            w_raw.append(raw)
+        nc.gpsimd.dma_start(gain[:], gn.rearrange("(p t) o -> p (t o)", t=PACK))
 
         d_picked_bytes = keep.tile([P, H], U8, name="d_picked_bytes", align_bytes=64)
         nc.vector.tensor_copy(d_picked_bytes[:], d_bytes[:].indirect(k1_t[:]))
-        d_dealt_bytes = keep.tile([P, H], U8, name="d_dealt_bytes", align_bytes=64)
+        d_dealt_bytes = keep.tile([P, H], U8, name="d_dealt_bytes", tag="w_raw0", align_bytes=64)
         nc.vector.tensor_copy(
-            d_dealt_bytes[:].rearrange("p (t m) -> p m t", t=PACK), d_picked_bytes[:].rearrange("p (m t) -> p m t", t=PACK)
+            d_dealt_bytes[:].rearrange("p (t m) -> p t m", t=PACK), d_picked_bytes[:].rearrange("p (m t) -> p t m", t=PACK)
         )
         d_plane = keep.tile([P, H], U8, name="d_plane", align_bytes=64)
         nc.vector.tensor_copy(d_plane[:].bitcast(I32), d_dealt_bytes[:].bitcast(I32))
         for a in range(1, 4):
             nc.scalar.dma_start(d_plane[a:P:32, :].bitcast(I32), d_dealt_bytes[8 * a : P : 32, :].bitcast(I32))
 
+        w_raw = keep.tile([P, PACK, N], F32, name="w_raw", tag="w_raw0", align_bytes=64)
+        nc.sync.dma_start(w_raw[:], w1.rearrange("(p j) m -> p j m", j=PACK))
+
         x_plane = keep.tile([P, S], U8, name="x_plane", align_bytes=64)
         nc.vector.tensor_copy(x_plane[:], x_bytes[:].indirect(offs_t[:]))
 
         d_picked = keep.tile([P, H], U32, name="d_picked", align_bytes=64)
         nc.vector.tensor_copy(d_picked[:], d_table[:].bitcast(U32).indirect(k1_t[:]))
-        d_codes = keep.tile([P, H], U32, name="d_codes", align_bytes=64)
+        d_codes = keep.tile([P, H], U32, name="d_codes", tag="d_codes", align_bytes=64)
         nc.vector.tensor_copy(
-            d_codes[:].bitcast(I32).rearrange("p (t m) -> p m t", t=PACK),
-            d_picked[:].bitcast(I32).rearrange("p (m t) -> p m t", t=PACK),
+            d_codes[:].bitcast(I32).rearrange("p (t a i) -> p a t i", t=PACK, i=4),
+            d_picked[:].bitcast(I32).rearrange("p (a i t) -> p a t i", t=PACK, i=4),
         )
         x_codes = keep.tile([P, S], U32, name="x_codes", align_bytes=64)
-        nc.vector.tensor_copy(x_codes[:], x_table[:].bitcast(U32).indirect(offs_t[:]))
+        halves = [slice(0, HALF), slice(HALF, S)]
+        for hf in range(2):
+            nc.vector.tensor_copy(x_codes[:, halves[hf]], x_table[:].bitcast(U32).indirect(offs_t[:, 16 * hf : 16 * hf + 16]))
 
-        h_acc = []
-        for t in range(PACK):
-            acc = psum.tile([P, S], F32, name=f"h_acc{t}")
+        def product(acc, lhs_codes, lhs_plane, t, rhs_codes, rhs_plane, part):
             cols = slice(t * P, (t + 1) * P)
             nc.tensor.matmul_mx(
-                out=acc[:], lhsT=d_codes[:, cols].bitcast(FP8X4), lhsT_scale=d_plane[:, cols],
-                rhs=x_codes[:].bitcast(FP8X4), rhs_scale=x_plane[:], start=True, stop=True,
+                out=acc, lhsT=lhs_codes[:, cols].bitcast(FP8X4), lhsT_scale=lhs_plane[:, cols],
+                rhs=rhs_codes[:, part].bitcast(FP8X4), rhs_scale=rhs_plane[:, part], start=True, stop=True,
             )
-            h_acc.append(acc)
 
-        w_bf = keep.tile([P, N * PACK], BF16, name="w_bf", align_bytes=64)
+        h_first = [psum.tile([P, HALF], F32, name=f"h_first{hf}", tag=f"bank{hf}") for hf in range(2)]
+        h_acc = [None] + [psum.tile([P, S], F32, name=f"h_acc{t}", tag=f"bank{t + 1}") for t in range(1, PACK)]
+        for hf in range(2):
+            product(h_first[hf][:], d_codes, d_plane, 0, x_codes, x_plane, halves[hf])
+            product(h_acc[1][:, halves[hf]], d_codes, d_plane, 1, x_codes, x_plane, halves[hf])
+        for t in range(2, PACK):
+            product(h_acc[t][:], d_codes, d_plane, t, x_codes, x_plane, slice(0, S))
+
+        h = [keep.tile([P, S], F32, name=f"h{t}") for t in range(PACK)]
+        q = [keep.tile([P, W], F32, name=f"q{t}", tag=f"q{t}", align_bytes=64) for t in range(PACK)]
+        ra = [keep.tile([P, W], F32, name=f"ra{t}") for t in range(PACK)]
+        z_pairs = keep.tile([P, 2, S, 2], BF16, name="z_pairs", align_bytes=64)
+
+        for t in range(PACK):
+            if t == 0:
+                nc.scalar.activation(h[0][:, halves[0]], h_first[0][:], ACT.Copy, scale=0.0625)
+                nc.vector.tensor_scalar(h[0][:, halves[1]], h_first[1][:], 0.0625, None, ALU.mult)
+            else:
+                nc.vector.tensor_scalar(h[t][:], h_acc[t][:], 0.0625, None, ALU.mult)
+            nc.scalar.activation(q[t][:], h[t][:].indirect(n2_t[:]), ACT.Copy, scale=-0.5)
+        for t in range(PACK):
+            if t == 0:
+                dd = keep.tile([P, W], F32, name="dd0", tag="d_codes", align_bytes=64)
+            else:
+                dd = keep.tile([P, W], F32, name=f"dd{t}")
+            nc.vector.tensor_tensor(dd[:], h[t][:].indirect(n1_t[:]), q[t][:], ALU.add)
+            nc.vector.scalar_tensor_tensor(ra[t][:], q[t][:], -1.0, dd[:], ALU.mult, ALU.min)
+            if t < PACK - 1:
+                nc.scalar.activation(h[t][:].indirect(n1_t[:]), ra[t][:], ACT.Copy)
+        w_bf = keep.tile([P, N * PACK], BF16, name="w_bf", tag="q0", align_bytes=64)
 
         def cast_w(hf):
             nc.vector.tensor_copy(
                 w_bf[:].rearrange("p (t a b j) -> p t a b j", t=PACK, b=8, j=PACK)[:, :, 8 * hf : 8 * hf + 8],
-                w_raw[hf][:].rearrange("p j (a t b) -> p t a b j", t=PACK, b=8),
+                w_raw[:].rearrange("p j (a t b) -> p t a b j", t=PACK, b=8)[:, :, 8 * hf : 8 * hf + 8],
             )
 
-        h = [keep.tile([P, S], F32, name=f"h{t}") for t in range(PACK)]
-        q = [keep.tile([P, W], F32, name=f"q{t}") for t in range(PACK)]
-        dd = [keep.tile([P, W], F32, name=f"dd{t}") for t in range(PACK)]
-        ra = [keep.tile([P, W], F32, name=f"ra{t}") for t in range(PACK)]
-        z_pairs = keep.tile([P, 2, S, 2], BF16, name="z_pairs", align_bytes=64)
+        def round_z(t, part=slice(0, S)):
+            nc.vector.tensor_scalar(z_pairs[:, t // 2, part, t % 2], h[t][:, part], gain[:, t : t + 1], None, ALU.mult)
 
-        def leave_scalar(t):
-            nc.scalar.activation(h[t][:], h_acc[t][:], ACT.Copy, scale=0.0625)
-
-        def leave_vector(t):
-            nc.vector.tensor_scalar(h[t][:], h_acc[t][:], 0.0625, None, ALU.mult)
-
-        def fetch_pa(t):
-            nc.scalar.activation(q[t][:], h[t][:].indirect(n2_t[:]), ACT.Copy, scale=-0.5)
-
-        def new_values(t):
-            nc.vector.tensor_tensor(dd[t][:], h[t][:].indirect(n1_t[:]), q[t][:], ALU.add)
-            nc.vector.scalar_tensor_tensor(ra[t][:], q[t][:], -1.0, dd[t][:], ALU.mult, ALU.min)
-
-        def put_scalar(t):
-            nc.scalar.activation(h[t][:].indirect(n1_t[:]), ra[t][:], ACT.Copy)
-
-        def put_vector(t):
-            nc.vector.tensor_copy(h[t][:].indirect(n1_t[:]), ra[t][:])
-
-        def round_z(t):
-            nc.vector.tensor_scalar(z_pairs[:, t // 2, :, t % 2], h[t][:], gain[:, t : t + 1], None, ALU.mult)
-
+        last = PACK - 1
+        nc.vector.tensor_copy(h[last][:].indirect(n1_t[:, : SPLIT // 16]), ra[last][:, :SPLIT])
+        nc.scalar.activation(h[last][:].indirect(n1_t[:, SPLIT // 16 :]), ra[last][:, SPLIT:], ACT.Copy)
         cast_w(0)
-        leave_scalar(0)
-        fetch_pa(0)
-        leave_vector(1)
-        fetch_pa(1)
-        leave_scalar(2)
-        new_values(0)
-        leave_vector(3)
-        fetch_pa(2)
-        fetch_pa(3)
-        new_values(1)
-        put_scalar(0)
-        new_values(2)
-        put_scalar(1)
-        new_values(3)
-        put_scalar(2)
-        put_vector(3)
         cast_w(1)
         w_codes = keep.tile([P, N], U32, name="w_codes", align_bytes=64)
         w_plane = keep.tile([P, N], U8, name="w_plane", align_bytes=64)
         round_z(0)
         nc.vector.quantize_mx(out=w_codes[:].bitcast(FP8X4), scales=w_plane[:], in_=w_bf[:])
         round_z(1)
-        round_z(3)
         round_z(2)
+        round_z(3, halves[0])
+        round_z(3, halves[1])
 
-        z_bf, z_codes, z_plane = [], [], []
+        z_bf = []
         for hf in range(2):
             zb = keep.tile([P, HALF * PACK], BF16, name=f"z_bf{hf}", align_bytes=64)
             nc.vector.tensor_copy(
                 zb[:].bitcast(F32).rearrange("p (c u) -> p c u", u=2),
-                z_pairs[:].rearrange("p u c e -> p u (c e)").bitcast(F32)[:, :, hf * HALF : (hf + 1) * HALF].rearrange("p u c -> p c u"),
+                z_pairs[:].rearrange("p u c e -> p u (c e)").bitcast(F32)[:, :, halves[hf]].rearrange("p u c -> p c u"),
             )
             z_bf.append(zb)
+        z_codes = keep.tile([P, S], U32, name="z_codes", align_bytes=64)
+        z_plane = keep.tile([P, S], U8, name="z_plane", align_bytes=64)
         for hf in range(2):
-            zc = keep.tile([P, HALF], U32, name=f"z_codes{hf}", align_bytes=64)
-            zs = keep.tile([P, HALF], U8, name=f"z_plane{hf}", align_bytes=64)
-            nc.vector.quantize_mx(out=zc[:].bitcast(FP8X4), scales=zs[:], in_=z_bf[hf][:])
-            z_codes.append(zc)
-            z_plane.append(zs)
+            nc.vector.quantize_mx(out=z_codes[:, halves[hf]].bitcast(FP8X4), scales=z_plane[:, halves[hf]], in_=z_bf[hf][:])
 
-        h2_acc = [psum.tile([P, S], F32, name=f"h2_acc{t}") for t in range(PACK)]
-        for t in range(PACK):
-            cols = slice(t * P, (t + 1) * P)
-            for hf in range(2):
-                nc.tensor.matmul_mx(
-                    out=h2_acc[t][:, hf * HALF : (hf + 1) * HALF], lhsT=w_codes[:, cols].bitcast(FP8X4), lhsT_scale=w_plane[:, cols],
-                    rhs=z_codes[hf][:].bitcast(FP8X4), rhs_scale=z_plane[hf][:], start=True, stop=True,
-                )
+        h2_first = [psum.tile([P, HALF], F32, name=f"h2_first{hf}", tag=f"bank{hf}") for hf in range(2)]
+        h2_acc = [None] + [psum.tile([P, S], F32, name=f"h2_acc{t}", tag=f"bank{t + 1}") for t in range(1, PACK)]
+        for hf in range(2):
+            product(h2_first[hf][:], w_codes, w_plane, 0, z_codes, z_plane, halves[hf])
+        for t in range(1, PACK):
+            product(h2_acc[t][:], w_codes, w_plane, t, z_codes, z_plane, slice(0, S))
 
         out_rows = out.rearrange("(a t b) n -> t a b n", t=PACK, b=8)
         h2 = [keep.tile([P, S], F32, name=f"h2_{t}") for t in range(PACK)]
-        for t in range(PACK):
+        for hf in range(2):
+            nc.vector.tensor_copy(h2[0][:, halves[hf]], h2_first[hf][:])
+        for t in range(1, PACK):
             nc.vector.tensor_copy(h2[t][:], h2_acc[t][:])
         for t in range(PACK):
-            for hf in range(2):
-                cols = slice(hf * HALF, (hf + 1) * HALF)
-                gate = keep.tile([P, HALF], F32, name=f"gate{t}_{hf}")
-                nc.scalar.activation(gate[:], h2[t][:].indirect(n3_t[:, 16 * hf : 16 * hf + 16]), ACT.Sigmoid)
-                res = keep.tile([P, HALF], F32, name=f"res{t}_{hf}")
-                nc.vector.tensor_tensor(res[:], h2[t][:, cols], gate[:], ALU.mult)
-                nc.sync.dma_start(out_rows[t, :, :, cols], res[:])
+            edges = [0, HALF, S] if t < last else [0, HALF, HALF + HALF // 2, S]
+            for lo, hi in zip(edges, edges[1:]):
+                gate = keep.tile([P, hi - lo], F32, name=f"gate{t}_{lo}")
+                nc.scalar.activation(gate[:], h2[t][:].indirect(n3_t[:, lo // 16 : hi // 16]), ACT.Sigmoid)
+                res = keep.tile([P, hi - lo], F32, name=f"res{t}_{lo}")
+                nc.vector.tensor_tensor(res[:], h2[t][:, lo:hi], gate[:], ALU.mult)
+                nc.sync.dma_start(out_rows[t, :, :, lo:hi], res[:])

@@ -18,7 +18,7 @@ ACT = mybir.ActivationFunctionType
 P = 128
 PACK = 4
 HALF = S // 2
-SPLIT = 192
+SPLIT = 320
 
 
 def tile_picked_pqlaykmingate_none_p_kernel(tc, x_words, x_scales, d_words, d_scales, gn, w1, offs, k1, n1, n2, n3, out):
@@ -40,37 +40,42 @@ def tile_picked_pqlaykmingate_none_p_kernel(tc, x_words, x_scales, d_words, d_sc
         x_table = keep.tile([P, T], I32, name="x_table", align_bytes=64)
         gain = keep.tile([P, PACK], F32, name="gain")
 
+        planes = keep.tile([P, H + S], U8, name="planes", align_bytes=64)
+        nc.vector.memset(d_bytes[:].bitcast(I32), 0)
+        nc.gpsimd.memset(x_bytes[:].bitcast(I32), 0)
+        nc.vector.memset(planes[:].bitcast(I32), 0)
+
+        def load_w(hf, tag):
+            raw = keep.tile([P, PACK, N // 2], F32, name=f"w_raw{hf}", tag=tag, align_bytes=64)
+            nc.sync.dma_start(raw[:], w1[:, hf * (N // 2) : (hf + 1) * (N // 2)].rearrange("(p j) m -> p j m", j=PACK))
+            return raw
+
         nc.sync.dma_start(k1_t[:], k1)
-        nc.sync.dma_start(d_bytes[:].bitcast(I32), d_scales[0].bitcast(I32).unsqueeze(1).to_broadcast([16, 8, G // 4]))
+        w_raw = [load_w(0, "w_raw0")]
         nc.sync.dma_start(offs_t[:], offs)
-        for q in range(4):
-            nc.sync.dma_start(
-                x_bytes[32 * q : 32 * q + 32, :].bitcast(I32),
-                x_scales[0, 4 * q : 4 * q + 4, :].bitcast(I32).unsqueeze(0).to_broadcast([8, 4, T // 4]),
-            )
-        nc.sync.dma_start(d_table[:], d_words[0].rearrange("p c r -> p (c r)").bitcast(I32))
         nc.sync.dma_start(n2_t[:], n2)
         nc.sync.dma_start(n1_t[:], n1)
+        nc.sync.dma_start(d_bytes[0:P:8, :].bitcast(I32), d_scales[0].bitcast(I32))
+        nc.sync.dma_start(x_bytes[0:P:8, :].bitcast(I32), x_scales[0].bitcast(I32))
+        nc.sync.dma_start(d_table[:], d_words[0].rearrange("p c r -> p (c r)").bitcast(I32))
         nc.sync.dma_start(x_table[:], x_words[0].rearrange("p c r -> p (c r)").bitcast(I32))
         nc.sync.dma_start(n3_t[:], n3)
         nc.gpsimd.dma_start(gain[:], gn.rearrange("(p t) o -> p (t o)", t=PACK))
 
         d_picked_bytes = keep.tile([P, H], U8, name="d_picked_bytes", align_bytes=64)
         nc.vector.tensor_copy(d_picked_bytes[:], d_bytes[:].indirect(k1_t[:]))
-        d_dealt_bytes = keep.tile([P, H], U8, name="d_dealt_bytes", tag="w_raw0", align_bytes=64)
+        staged = keep.tile([P, H + S], U8, name="staged", align_bytes=64)
         nc.vector.tensor_copy(
-            d_dealt_bytes[:].rearrange("p (t m) -> p t m", t=PACK), d_picked_bytes[:].rearrange("p (m t) -> p t m", t=PACK)
+            staged[:, :H].rearrange("p (t m) -> p t m", t=PACK), d_picked_bytes[:].rearrange("p (m t) -> p t m", t=PACK)
         )
-        d_plane = keep.tile([P, H], U8, name="d_plane", align_bytes=64)
-        nc.vector.tensor_copy(d_plane[:].bitcast(I32), d_dealt_bytes[:].bitcast(I32))
-        for a in range(1, 4):
-            nc.scalar.dma_start(d_plane[a:P:32, :].bitcast(I32), d_dealt_bytes[8 * a : P : 32, :].bitcast(I32))
-
-        w_raw = keep.tile([P, PACK, N], F32, name="w_raw", tag="w_raw0", align_bytes=64)
-        nc.sync.dma_start(w_raw[:], w1.rearrange("(p j) m -> p j m", j=PACK))
-
-        x_plane = keep.tile([P, S], U8, name="x_plane", align_bytes=64)
-        nc.vector.tensor_copy(x_plane[:], x_bytes[:].indirect(offs_t[:]))
+        x_picked_bytes = keep.tile([P, S], U8, name="x_picked_bytes", tag="w_raw1", align_bytes=64)
+        nc.vector.tensor_copy(x_picked_bytes[:], x_bytes[:].indirect(offs_t[:]))
+        nc.vector.tensor_copy(staged[:, H:].bitcast(I32), x_picked_bytes[:].bitcast(I32))
+        for a in range(4):
+            nc.sync.dma_start(planes[a:P:32, :].bitcast(I32), staged[8 * a : P : 32, :].bitcast(I32))
+        d_plane = planes[:, :H]
+        x_plane = planes[:, H:]
+        w_raw.append(load_w(1, "w_raw1"))
 
         d_picked = keep.tile([P, H], U32, name="d_picked", align_bytes=64)
         nc.vector.tensor_copy(d_picked[:], d_table[:].bitcast(U32).indirect(k1_t[:]))
@@ -102,30 +107,36 @@ def tile_picked_pqlaykmingate_none_p_kernel(tc, x_words, x_scales, d_words, d_sc
         h = [keep.tile([P, S], F32, name=f"h{t}") for t in range(PACK)]
         q = [keep.tile([P, W], F32, name=f"q{t}", tag=f"q{t}", align_bytes=64) for t in range(PACK)]
         ra = [keep.tile([P, W], F32, name=f"ra{t}") for t in range(PACK)]
-        z_pairs = keep.tile([P, 2, S, 2], BF16, name="z_pairs", align_bytes=64)
 
-        for t in range(PACK):
-            if t == 0:
-                nc.scalar.activation(h[0][:, halves[0]], h_first[0][:], ACT.Copy, scale=0.0625)
-                nc.vector.tensor_scalar(h[0][:, halves[1]], h_first[1][:], 0.0625, None, ALU.mult)
-            else:
-                nc.vector.tensor_scalar(h[t][:], h_acc[t][:], 0.0625, None, ALU.mult)
+        dd = []
+
+        def fetch_pa(t):
             nc.scalar.activation(q[t][:], h[t][:].indirect(n2_t[:]), ACT.Copy, scale=-0.5)
-        for t in range(PACK):
-            if t == 0:
-                dd = keep.tile([P, W], F32, name="dd0", tag="d_codes", align_bytes=64)
-            else:
-                dd = keep.tile([P, W], F32, name=f"dd{t}")
-            nc.vector.tensor_tensor(dd[:], h[t][:].indirect(n1_t[:]), q[t][:], ALU.add)
-            nc.vector.scalar_tensor_tensor(ra[t][:], q[t][:], -1.0, dd[:], ALU.mult, ALU.min)
+
+        def fetch_old(t):
+            dd.append(keep.tile([P, W], F32, name=f"dd{t}", tag="q1" if t == 3 else "dd", align_bytes=64))
+            nc.vector.tensor_tensor(dd[t][:], h[t][:].indirect(n1_t[:]), q[t][:], ALU.add)
+
+        def smaller(t):
+            nc.vector.scalar_tensor_tensor(ra[t][:], q[t][:], -1.0, dd[t][:], ALU.mult, ALU.min)
             if t < PACK - 1:
                 nc.scalar.activation(h[t][:].indirect(n1_t[:]), ra[t][:], ACT.Copy)
-        w_bf = keep.tile([P, N * PACK], BF16, name="w_bf", tag="q0", align_bytes=64)
+
+        nc.scalar.activation(h[0][:, halves[0]], h_first[0][:], ACT.Copy, scale=0.0625)
+        nc.vector.tensor_scalar(h[0][:, halves[1]], h_first[1][:], 0.0625, None, ALU.mult)
+        for t in range(1, PACK):
+            nc.vector.tensor_scalar(h[t][:], h_acc[t][:], 0.0625, None, ALU.mult)
+        for t in range(PACK):
+            fetch_pa(t)
+        for t in range(PACK):
+            fetch_old(t)
+            smaller(t)
+        w_bf = keep.tile([P, N * PACK], BF16, name="w_bf", align_bytes=64)
 
         def cast_w(hf):
-            nc.vector.tensor_copy(
+            (nc.scalar.copy if hf == 0 else nc.vector.tensor_copy)(
                 w_bf[:].rearrange("p (t a b j) -> p t a b j", t=PACK, b=8, j=PACK)[:, :, 8 * hf : 8 * hf + 8],
-                w_raw[:].rearrange("p j (a t b) -> p t a b j", t=PACK, b=8)[:, :, 8 * hf : 8 * hf + 8],
+                w_raw[hf][:].rearrange("p j (a t b) -> p t a b j", t=PACK, b=8),
             )
 
         def round_z(t, part=slice(0, S)):
@@ -138,6 +149,7 @@ def tile_picked_pqlaykmingate_none_p_kernel(tc, x_words, x_scales, d_words, d_sc
         cast_w(1)
         w_codes = keep.tile([P, N], U32, name="w_codes", align_bytes=64)
         w_plane = keep.tile([P, N], U8, name="w_plane", align_bytes=64)
+        z_pairs = keep.tile([P, 2, S, 2], BF16, name="z_pairs", tag="q3", align_bytes=64)
         round_z(0)
         nc.vector.quantize_mx(out=w_codes[:].bitcast(FP8X4), scales=w_plane[:], in_=w_bf[:])
         round_z(1)

@@ -17,8 +17,12 @@ ACT = mybir.ActivationFunctionType
 
 P = 128
 PACK = 4
+GROUP = 16
+BLOCK_ROWS = 8
+QUADRANT = 32
+LINE = 4
 HALF = S // 2
-SPLIT = 320
+SPLIT = 288
 
 
 def tile_picked_pqlaykmingate_none_p_kernel(tc, x_words, x_scales, d_words, d_scales, gn, w1, offs, k1, n1, n2, n3, out):
@@ -28,11 +32,11 @@ def tile_picked_pqlaykmingate_none_p_kernel(tc, x_words, x_scales, d_words, d_sc
         keep = ctx.enter_context(tc.tile_pool(name="keep", bufs=1))
         psum = ctx.enter_context(tc.psum_pool(name="psum", bufs=1))
 
-        k1_t = lists.tile([P, H // 16], U16, name="k1_t")
-        offs_t = lists.tile([P, S // 16], U16, name="offs_t")
-        n1_t = lists.tile([P, W // 16], U16, name="n1_t")
-        n2_t = lists.tile([P, W // 16], U16, name="n2_t")
-        n3_t = lists.tile([P, S // 16], U16, name="n3_t")
+        k1_t = lists.tile([P, H // GROUP], U16, name="k1_t")
+        offs_t = lists.tile([P, S // GROUP], U16, name="offs_t")
+        n1_t = lists.tile([P, W // GROUP], U16, name="n1_t")
+        n2_t = lists.tile([P, W // GROUP], U16, name="n2_t")
+        n3_t = lists.tile([P, S // GROUP], U16, name="n3_t")
 
         d_bytes = keep.tile([P, G], U8, name="d_bytes", align_bytes=64)
         x_bytes = keep.tile([P, T], U8, name="x_bytes", align_bytes=64)
@@ -55,8 +59,8 @@ def tile_picked_pqlaykmingate_none_p_kernel(tc, x_words, x_scales, d_words, d_sc
         nc.sync.dma_start(offs_t[:], offs)
         nc.sync.dma_start(n2_t[:], n2)
         nc.sync.dma_start(n1_t[:], n1)
-        nc.sync.dma_start(d_bytes[0:P:8, :].bitcast(I32), d_scales[0].bitcast(I32))
-        nc.sync.dma_start(x_bytes[0:P:8, :].bitcast(I32), x_scales[0].bitcast(I32))
+        nc.sync.dma_start(d_bytes[0:P:BLOCK_ROWS, :].bitcast(I32), d_scales[0].bitcast(I32))
+        nc.sync.dma_start(x_bytes[0:P:BLOCK_ROWS, :].bitcast(I32), x_scales[0].bitcast(I32))
         nc.sync.dma_start(d_table[:], d_words[0].rearrange("p c r -> p (c r)").bitcast(I32))
         nc.sync.dma_start(x_table[:], x_words[0].rearrange("p c r -> p (c r)").bitcast(I32))
         nc.sync.dma_start(n3_t[:], n3)
@@ -68,26 +72,26 @@ def tile_picked_pqlaykmingate_none_p_kernel(tc, x_words, x_scales, d_words, d_sc
         nc.vector.tensor_copy(
             staged[:, :H].rearrange("p (t m) -> p t m", t=PACK), d_picked_bytes[:].rearrange("p (m t) -> p t m", t=PACK)
         )
-        x_picked_bytes = keep.tile([P, S], U8, name="x_picked_bytes", tag="w_raw1", align_bytes=64)
+        x_picked_bytes = keep.tile([P, S], U8, name="x_picked_bytes", align_bytes=64)
         nc.vector.tensor_copy(x_picked_bytes[:], x_bytes[:].indirect(offs_t[:]))
         nc.vector.tensor_copy(staged[:, H:].bitcast(I32), x_picked_bytes[:].bitcast(I32))
-        for a in range(4):
-            nc.sync.dma_start(planes[a:P:32, :].bitcast(I32), staged[8 * a : P : 32, :].bitcast(I32))
+        for r in range(QUADRANT // BLOCK_ROWS):
+            nc.sync.dma_start(planes[r:P:QUADRANT, :].bitcast(I32), staged[BLOCK_ROWS * r : P : QUADRANT, :].bitcast(I32))
         d_plane = planes[:, :H]
         x_plane = planes[:, H:]
-        w_raw.append(load_w(1, "w_raw1"))
 
         d_picked = keep.tile([P, H], U32, name="d_picked", align_bytes=64)
         nc.vector.tensor_copy(d_picked[:], d_table[:].bitcast(U32).indirect(k1_t[:]))
         d_codes = keep.tile([P, H], U32, name="d_codes", tag="d_codes", align_bytes=64)
         nc.vector.tensor_copy(
-            d_codes[:].bitcast(I32).rearrange("p (t a i) -> p a t i", t=PACK, i=4),
-            d_picked[:].bitcast(I32).rearrange("p (a i t) -> p a t i", t=PACK, i=4),
+            d_codes[:].bitcast(I32).rearrange("p (t a i) -> p a t i", t=PACK, i=LINE),
+            d_picked[:].bitcast(I32).rearrange("p (a i t) -> p a t i", t=PACK, i=LINE),
         )
         x_codes = keep.tile([P, S], U32, name="x_codes", align_bytes=64)
         halves = [slice(0, HALF), slice(HALF, S)]
-        for hf in range(2):
-            nc.vector.tensor_copy(x_codes[:, halves[hf]], x_table[:].bitcast(U32).indirect(offs_t[:, 16 * hf : 16 * hf + 16]))
+        for part in halves:
+            entries = offs_t[:, part.start // GROUP : part.stop // GROUP]
+            nc.vector.tensor_copy(x_codes[:, part], x_table[:].bitcast(U32).indirect(entries))
 
         def product(acc, lhs_codes, lhs_plane, t, rhs_codes, rhs_plane, part):
             cols = slice(t * P, (t + 1) * P)
@@ -97,65 +101,56 @@ def tile_picked_pqlaykmingate_none_p_kernel(tc, x_words, x_scales, d_words, d_sc
             )
 
         h_first = [psum.tile([P, HALF], F32, name=f"h_first{hf}", tag=f"bank{hf}") for hf in range(2)]
-        h_acc = [None] + [psum.tile([P, S], F32, name=f"h_acc{t}", tag=f"bank{t + 1}") for t in range(1, PACK)]
+        h_acc = {t: psum.tile([P, S], F32, name=f"h_acc{t}", tag=f"bank{t + 1}") for t in range(1, PACK)}
         for hf in range(2):
             product(h_first[hf][:], d_codes, d_plane, 0, x_codes, x_plane, halves[hf])
             product(h_acc[1][:, halves[hf]], d_codes, d_plane, 1, x_codes, x_plane, halves[hf])
         for t in range(2, PACK):
             product(h_acc[t][:], d_codes, d_plane, t, x_codes, x_plane, slice(0, S))
 
+        w_raw.append(load_w(1, "d_codes"))
         h = [keep.tile([P, S], F32, name=f"h{t}") for t in range(PACK)]
         q = [keep.tile([P, W], F32, name=f"q{t}", tag=f"q{t}", align_bytes=64) for t in range(PACK)]
         ra = [keep.tile([P, W], F32, name=f"ra{t}") for t in range(PACK)]
-
-        dd = []
-
-        def fetch_pa(t):
-            nc.scalar.activation(q[t][:], h[t][:].indirect(n2_t[:]), ACT.Copy, scale=-0.5)
-
-        def fetch_old(t):
-            dd.append(keep.tile([P, W], F32, name=f"dd{t}", tag="q1" if t == 3 else "dd", align_bytes=64))
-            nc.vector.tensor_tensor(dd[t][:], h[t][:].indirect(n1_t[:]), q[t][:], ALU.add)
-
-        def smaller(t):
-            nc.vector.scalar_tensor_tensor(ra[t][:], q[t][:], -1.0, dd[t][:], ALU.mult, ALU.min)
-            if t < PACK - 1:
-                nc.scalar.activation(h[t][:].indirect(n1_t[:]), ra[t][:], ACT.Copy)
+        last = PACK - 1
 
         nc.scalar.activation(h[0][:, halves[0]], h_first[0][:], ACT.Copy, scale=0.0625)
         nc.vector.tensor_scalar(h[0][:, halves[1]], h_first[1][:], 0.0625, None, ALU.mult)
         for t in range(1, PACK):
             nc.vector.tensor_scalar(h[t][:], h_acc[t][:], 0.0625, None, ALU.mult)
         for t in range(PACK):
-            fetch_pa(t)
+            nc.scalar.activation(q[t][:], h[t][:].indirect(n2_t[:]), ACT.Copy, scale=-0.5)
         for t in range(PACK):
-            fetch_old(t)
-            smaller(t)
+            dd = keep.tile([P, W], F32, name=f"dd{t}", tag="q1" if t == last else "dd", align_bytes=64)
+            nc.vector.tensor_tensor(dd[:], h[t][:].indirect(n1_t[:]), q[t][:], ALU.add)
+            nc.vector.scalar_tensor_tensor(ra[t][:], q[t][:], -1.0, dd[:], ALU.mult, ALU.min)
+            if t < last:
+                nc.scalar.activation(h[t][:].indirect(n1_t[:]), ra[t][:], ACT.Copy)
         w_bf = keep.tile([P, N * PACK], BF16, name="w_bf", align_bytes=64)
+        nc.vector.tensor_copy(h[last][:].indirect(n1_t[:, : SPLIT // GROUP]), ra[last][:, :SPLIT])
+        nc.scalar.activation(h[last][:].indirect(n1_t[:, SPLIT // GROUP :]), ra[last][:, SPLIT:], ACT.Copy)
 
-        def cast_w(hf):
-            (nc.scalar.copy if hf == 0 else nc.vector.tensor_copy)(
-                w_bf[:].rearrange("p (t a b j) -> p t a b j", t=PACK, b=8, j=PACK)[:, :, 8 * hf : 8 * hf + 8],
-                w_raw[hf][:].rearrange("p j (a t b) -> p t a b j", t=PACK, b=8),
+        w_dealt = w_bf[:].rearrange("p (t a b j) -> p t a b j", t=PACK, b=BLOCK_ROWS, j=PACK)
+        a_half = N // QUADRANT // 2
+        for hf, copy in enumerate((nc.scalar.copy, nc.vector.tensor_copy)):
+            copy(
+                w_dealt[:, :, a_half * hf : a_half * (hf + 1)],
+                w_raw[hf][:].rearrange("p j (a t b) -> p t a b j", t=PACK, b=BLOCK_ROWS),
             )
-
-        def round_z(t, part=slice(0, S)):
-            nc.vector.tensor_scalar(z_pairs[:, t // 2, part, t % 2], h[t][:, part], gain[:, t : t + 1], None, ALU.mult)
-
-        last = PACK - 1
-        nc.vector.tensor_copy(h[last][:].indirect(n1_t[:, : SPLIT // 16]), ra[last][:, :SPLIT])
-        nc.scalar.activation(h[last][:].indirect(n1_t[:, SPLIT // 16 :]), ra[last][:, SPLIT:], ACT.Copy)
-        cast_w(0)
-        cast_w(1)
         w_codes = keep.tile([P, N], U32, name="w_codes", align_bytes=64)
         w_plane = keep.tile([P, N], U8, name="w_plane", align_bytes=64)
+
         z_pairs = keep.tile([P, 2, S, 2], BF16, name="z_pairs", tag="q3", align_bytes=64)
-        round_z(0)
+
+        def round_z(t, part):
+            nc.vector.tensor_scalar(z_pairs[:, t // 2, part, t % 2], h[t][:, part], gain[:, t : t + 1], None, ALU.mult)
+
+        round_z(0, slice(0, S))
         nc.vector.quantize_mx(out=w_codes[:].bitcast(FP8X4), scales=w_plane[:], in_=w_bf[:])
-        round_z(1)
-        round_z(2)
-        round_z(3, halves[0])
-        round_z(3, halves[1])
+        for t in range(1, last):
+            round_z(t, slice(0, S))
+        for part in halves:
+            round_z(last, part)
 
         z_bf = []
         for hf in range(2):
@@ -171,13 +166,13 @@ def tile_picked_pqlaykmingate_none_p_kernel(tc, x_words, x_scales, d_words, d_sc
             nc.vector.quantize_mx(out=z_codes[:, halves[hf]].bitcast(FP8X4), scales=z_plane[:, halves[hf]], in_=z_bf[hf][:])
 
         h2_first = [psum.tile([P, HALF], F32, name=f"h2_first{hf}", tag=f"bank{hf}") for hf in range(2)]
-        h2_acc = [None] + [psum.tile([P, S], F32, name=f"h2_acc{t}", tag=f"bank{t + 1}") for t in range(1, PACK)]
+        h2_acc = {t: psum.tile([P, S], F32, name=f"h2_acc{t}", tag=f"bank{t + 1}") for t in range(1, PACK)}
         for hf in range(2):
             product(h2_first[hf][:], w_codes, w_plane, 0, z_codes, z_plane, halves[hf])
         for t in range(1, PACK):
             product(h2_acc[t][:], w_codes, w_plane, t, z_codes, z_plane, slice(0, S))
 
-        out_rows = out.rearrange("(a t b) n -> t a b n", t=PACK, b=8)
+        out_rows = out.rearrange("(a t b) n -> t a b n", t=PACK, b=BLOCK_ROWS)
         h2 = [keep.tile([P, S], F32, name=f"h2_{t}") for t in range(PACK)]
         for hf in range(2):
             nc.vector.tensor_copy(h2[0][:, halves[hf]], h2_first[hf][:])
@@ -187,7 +182,7 @@ def tile_picked_pqlaykmingate_none_p_kernel(tc, x_words, x_scales, d_words, d_sc
             edges = [0, HALF, S] if t < last else [0, HALF, HALF + HALF // 2, S]
             for lo, hi in zip(edges, edges[1:]):
                 gate = keep.tile([P, hi - lo], F32, name=f"gate{t}_{lo}")
-                nc.scalar.activation(gate[:], h2[t][:].indirect(n3_t[:, lo // 16 : hi // 16]), ACT.Sigmoid)
+                nc.scalar.activation(gate[:], h2[t][:].indirect(n3_t[:, lo // GROUP : hi // GROUP]), ACT.Sigmoid)
                 res = keep.tile([P, hi - lo], F32, name=f"res{t}_{lo}")
                 nc.vector.tensor_tensor(res[:], h2[t][:, lo:hi], gate[:], ALU.mult)
                 nc.sync.dma_start(out_rows[t, :, :, lo:hi], res[:])

from contextlib import ExitStack

import concourse.mybir as mybir

K, T, S, N, G, H, W = 512, 2048, 512, 512, 2048, 512, 384
FLOPS = 2 * K * H * S + 2 * H * N * S

F32 = mybir.dt.float32
BF16 = mybir.dt.bfloat16
I32 = mybir.dt.int32
U32 = mybir.dt.uint32
U16 = mybir.dt.uint16
U8 = mybir.dt.uint8
FP8X4 = mybir.dt.float8_e4m3fn_x4
ALU = mybir.AluOpType
ACT = mybir.ActivationFunctionType

P = 128
PACK = 4
GROUP = 16
BLOCK_ROWS = 8
QUADRANT = 32
LINE = 4
HALF = S // 2
SPLIT = 288


def tile_picked_pqlaykmingate_none_p_kernel(tc, x_words, x_scales, d_words, d_scales, gn, w1, offs, k1, n1, n2, n3, out):
    nc = tc.nc
    with ExitStack() as ctx:
        lists = ctx.enter_context(tc.tile_pool(name="lists", bufs=1))
        keep = ctx.enter_context(tc.tile_pool(name="keep", bufs=1))
        psum = ctx.enter_context(tc.psum_pool(name="psum", bufs=1))

        k1_t = lists.tile([P, H // GROUP], U16, name="k1_t")
        offs_t = lists.tile([P, S // GROUP], U16, name="offs_t")
        n1_t = lists.tile([P, W // GROUP], U16, name="n1_t")
        n2_t = lists.tile([P, W // GROUP], U16, name="n2_t")
        n3_t = lists.tile([P, S // GROUP], U16, name="n3_t")

        d_bytes = keep.tile([P, G], U8, name="d_bytes", align_bytes=64)
        x_bytes = keep.tile([P, T], U8, name="x_bytes", align_bytes=64)
        d_table = keep.tile([P, G], I32, name="d_table", align_bytes=64)
        x_table = keep.tile([P, T], I32, name="x_table", align_bytes=64)
        gain = keep.tile([P, PACK], F32, name="gain")

        planes = keep.tile([P, H + S], U8, name="planes", align_bytes=64)
        nc.vector.memset(d_bytes[:].bitcast(I32), 0)
        nc.gpsimd.memset(x_bytes[:].bitcast(I32), 0)
        nc.vector.memset(planes[:].bitcast(I32), 0)

        def load_w(hf, tag):
            raw = keep.tile([P, PACK, N // 2], F32, name=f"w_raw{hf}", tag=tag, align_bytes=64)
            nc.sync.dma_start(raw[:], w1[:, hf * (N // 2) : (hf + 1) * (N // 2)].rearrange("(p j) m -> p j m", j=PACK))
            return raw

        nc.sync.dma_start(k1_t[:], k1)
        w_raw = [load_w(0, "w_raw0")]
        nc.sync.dma_start(offs_t[:], offs)
        nc.sync.dma_start(n2_t[:], n2)
        nc.sync.dma_start(n1_t[:], n1)
        nc.sync.dma_start(d_bytes[0:P:BLOCK_ROWS, :].bitcast(I32), d_scales[0].bitcast(I32))
        nc.sync.dma_start(x_bytes[0:P:BLOCK_ROWS, :].bitcast(I32), x_scales[0].bitcast(I32))
        nc.sync.dma_start(d_table[:], d_words[0].rearrange("p c r -> p (c r)").bitcast(I32))
        nc.sync.dma_start(x_table[:], x_words[0].rearrange("p c r -> p (c r)").bitcast(I32))
        nc.sync.dma_start(n3_t[:], n3)
        nc.gpsimd.dma_start(gain[:], gn.rearrange("(p t) o -> p (t o)", t=PACK))

        d_picked_bytes = keep.tile([P, H], U8, name="d_picked_bytes", align_bytes=64)
        nc.vector.tensor_copy(d_picked_bytes[:], d_bytes[:].indirect(k1_t[:]))
        staged = keep.tile([P, H + S], U8, name="staged", align_bytes=64)
        nc.vector.tensor_copy(
            staged[:, :H].rearrange("p (t m) -> p t m", t=PACK), d_picked_bytes[:].rearrange("p (m t) -> p t m", t=PACK)
        )
        x_picked_bytes = keep.tile([P, S], U8, name="x_picked_bytes", align_bytes=64)
        nc.vector.tensor_copy(x_picked_bytes[:], x_bytes[:].indirect(offs_t[:]))
        nc.vector.tensor_copy(staged[:, H:].bitcast(I32), x_picked_bytes[:].bitcast(I32))
        for r in range(QUADRANT // BLOCK_ROWS):
            nc.sync.dma_start(planes[r:P:QUADRANT, :].bitcast(I32), staged[BLOCK_ROWS * r : P : QUADRANT, :].bitcast(I32))
        d_plane = planes[:, :H]
        x_plane = planes[:, H:]

        d_picked = keep.tile([P, H], U32, name="d_picked", align_bytes=64)
        nc.vector.tensor_copy(d_picked[:], d_table[:].bitcast(U32).indirect(k1_t[:]))
        d_codes = keep.tile([P, H], U32, name="d_codes", tag="d_codes", align_bytes=64)
        nc.vector.tensor_copy(
            d_codes[:].bitcast(I32).rearrange("p (t a i) -> p a t i", t=PACK, i=LINE),
            d_picked[:].bitcast(I32).rearrange("p (a i t) -> p a t i", t=PACK, i=LINE),
        )
        x_codes = keep.tile([P, S], U32, name="x_codes", align_bytes=64)
        halves = [slice(0, HALF), slice(HALF, S)]
        for part in halves:
            entries = offs_t[:, part.start // GROUP : part.stop // GROUP]
            nc.vector.tensor_copy(x_codes[:, part], x_table[:].bitcast(U32).indirect(entries))

        def product(acc, lhs_codes, lhs_plane, t, rhs_codes, rhs_plane, part):
            cols = slice(t * P, (t + 1) * P)
            nc.tensor.matmul_mx(
                out=acc, lhsT=lhs_codes[:, cols].bitcast(FP8X4), lhsT_scale=lhs_plane[:, cols],
                rhs=rhs_codes[:, part].bitcast(FP8X4), rhs_scale=rhs_plane[:, part], start=True, stop=True,
            )

        h_first = [psum.tile([P, HALF], F32, name=f"h_first{hf}", tag=f"bank{hf}") for hf in range(2)]
        h_acc = {t: psum.tile([P, S], F32, name=f"h_acc{t}", tag=f"bank{t + 1}") for t in range(1, PACK)}
        for hf in range(2):
            product(h_first[hf][:], d_codes, d_plane, 0, x_codes, x_plane, halves[hf])
            product(h_acc[1][:, halves[hf]], d_codes, d_plane, 1, x_codes, x_plane, halves[hf])
        for t in range(2, PACK):
            product(h_acc[t][:], d_codes, d_plane, t, x_codes, x_plane, slice(0, S))

        w_raw.append(load_w(1, "d_codes"))
        h = [keep.tile([P, S], F32, name=f"h{t}") for t in range(PACK)]
        q = [keep.tile([P, W], F32, name=f"q{t}", tag=f"q{t}", align_bytes=64) for t in range(PACK)]
        ra = [keep.tile([P, W], F32, name=f"ra{t}") for t in range(PACK)]
        last = PACK - 1

        nc.scalar.activation(h[0][:, halves[0]], h_first[0][:], ACT.Copy, scale=0.0625)
        nc.vector.tensor_scalar(h[0][:, halves[1]], h_first[1][:], 0.0625, None, ALU.mult)
        for t in range(1, PACK):
            nc.vector.tensor_scalar(h[t][:], h_acc[t][:], 0.0625, None, ALU.mult)
        for t in range(PACK):
            nc.scalar.activation(q[t][:], h[t][:].indirect(n2_t[:]), ACT.Copy, scale=-0.5)
        for t in range(PACK):
            dd = keep.tile([P, W], F32, name=f"dd{t}", tag="q1" if t == last else "dd", align_bytes=64)
            nc.vector.tensor_tensor(dd[:], h[t][:].indirect(n1_t[:]), q[t][:], ALU.add)
            nc.vector.scalar_tensor_tensor(ra[t][:], q[t][:], -1.0, dd[:], ALU.mult, ALU.min)
            if t < last:
                nc.scalar.activation(h[t][:].indirect(n1_t[:]), ra[t][:], ACT.Copy)
        w_bf = keep.tile([P, N * PACK], BF16, name="w_bf", align_bytes=64)
        nc.vector.tensor_copy(h[last][:].indirect(n1_t[:, : SPLIT // GROUP]), ra[last][:, :SPLIT])
        nc.scalar.activation(h[last][:].indirect(n1_t[:, SPLIT // GROUP :]), ra[last][:, SPLIT:], ACT.Copy)

        w_dealt = w_bf[:].rearrange("p (t a b j) -> p t a b j", t=PACK, b=BLOCK_ROWS, j=PACK)
        a_half = N // QUADRANT // 2
        for hf, copy in enumerate((nc.scalar.copy, nc.vector.tensor_copy)):
            copy(
                w_dealt[:, :, a_half * hf : a_half * (hf + 1)],
                w_raw[hf][:].rearrange("p j (a t b) -> p t a b j", t=PACK, b=BLOCK_ROWS),
            )
        w_codes = keep.tile([P, N], U32, name="w_codes", align_bytes=64)
        w_plane = keep.tile([P, N], U8, name="w_plane", align_bytes=64)

        z_pairs = keep.tile([P, 2, S, 2], BF16, name="z_pairs", tag="q3", align_bytes=64)

        def round_z(t, part):
            nc.vector.tensor_scalar(z_pairs[:, t // 2, part, t % 2], h[t][:, part], gain[:, t : t + 1], None, ALU.mult)

        round_z(0, slice(0, S))
        nc.vector.quantize_mx(out=w_codes[:].bitcast(FP8X4), scales=w_plane[:], in_=w_bf[:])
        for t in range(1, last):
            round_z(t, slice(0, S))
        for part in halves:
            round_z(last, part)

        z_bf = []
        for hf in range(2):
            zb = keep.tile([P, HALF * PACK], BF16, name=f"z_bf{hf}", align_bytes=64)
            nc.vector.tensor_copy(
                zb[:].bitcast(F32).rearrange("p (c u) -> p c u", u=2),
                z_pairs[:].rearrange("p u c e -> p u (c e)").bitcast(F32)[:, :, halves[hf]].rearrange("p u c -> p c u"),
            )
            z_bf.append(zb)
        z_codes = keep.tile([P, S], U32, name="z_codes", align_bytes=64)
        z_plane = keep.tile([P, S], U8, name="z_plane", align_bytes=64)
        for hf in range(2):
            nc.vector.quantize_mx(out=z_codes[:, halves[hf]].bitcast(FP8X4), scales=z_plane[:, halves[hf]], in_=z_bf[hf][:])

        h2_first = [psum.tile([P, HALF], F32, name=f"h2_first{hf}", tag=f"bank{hf}") for hf in range(2)]
        h2_acc = {t: psum.tile([P, S], F32, name=f"h2_acc{t}", tag=f"bank{t + 1}") for t in range(1, PACK)}
        for hf in range(2):
            product(h2_first[hf][:], w_codes, w_plane, 0, z_codes, z_plane, halves[hf])
        for t in range(1, PACK):
            product(h2_acc[t][:], w_codes, w_plane, t, z_codes, z_plane, slice(0, S))

        out_rows = out.rearrange("(a t b) n -> t a b n", t=PACK, b=BLOCK_ROWS)
        h2 = [keep.tile([P, S], F32, name=f"h2_{t}") for t in range(PACK)]
        for hf in range(2):
            nc.vector.tensor_copy(h2[0][:, halves[hf]], h2_first[hf][:])
        for t in range(1, PACK):
            nc.vector.tensor_copy(h2[t][:], h2_acc[t][:])
        for t in range(PACK):
            edges = [0, HALF, S] if t < last else [0, HALF, HALF + HALF // 2, S]
            for lo, hi in zip(edges, edges[1:]):
                gate = keep.tile([P, hi - lo], F32, name=f"gate{t}_{lo}")
                nc.scalar.activation(gate[:], h2[t][:].indirect(n3_t[:, lo // GROUP : hi // GROUP]), ACT.Sigmoid)
                res = keep.tile([P, hi - lo], F32, name=f"res{t}_{lo}")
                nc.vector.tensor_tensor(res[:], h2[t][:, lo:hi], gate[:], ALU.mult)
                nc.sync.dma_start(out_rows[t, :, :, lo:hi], res[:])
